import numpy as np
import ml_dtypes


def mxq(x, axis, fmt="e4m3"):
    dtype, down = {"e4m3": (ml_dtypes.float8_e4m3fn, 7), "e5m2": (ml_dtypes.float8_e5m2, 14)}[fmt]
    v = np.moveaxis(np.asarray(x, np.float32).astype(ml_dtypes.bfloat16).astype(np.float64), axis, -1)
    blocks = v.reshape(v.shape[:-1] + (-1, 32))
    amax = np.abs(blocks).max(-1, keepdims=True)
    byte = np.maximum(np.where(amax > 0, np.frexp(amax)[1] - 1 + 127, 0) - down, 1)
    scale = np.exp2(byte - 127.0)
    codes = (blocks / scale).astype(np.float32).astype(dtype).astype(np.float64)
    return np.moveaxis((codes * scale).reshape(v.shape), -1, axis)


WIDE = False


def mx_kscale(k):
    if not WIDE:
        return np.ones(k)
    levels = np.array([10, -10, 5, -5, 0])
    if k % 512:
        return np.exp2(np.random.permutation(np.resize(levels, k // 32))).repeat(32)
    a = np.empty((k // 512, 16))
    for p in range(k // 512):
        a[p, :8] = np.random.permutation(np.resize(levels, 8))
        for g in range(8):
            far = levels[np.abs(levels - a[p, g]) >= 10]
            a[p, g + 8] = far[np.random.randint(len(far))]
    return np.exp2(a.ravel()).repeat(32)


def f64(x):
    return np.asarray(x).astype(np.float64)


def striped(idx):
    return np.tile(np.asarray(idx).reshape(-1, 16).T, (8, 1)).astype(np.uint16)


def unstriped(offs):
    return offs[:16].T.reshape(-1).astype(np.int64)


E2M1 = np.array([0.0, 0.5, 1.0, 1.5, 2.0, 3.0, 4.0, 6.0, -0.0, -0.5, -1.0, -1.5, -2.0, -3.0, -4.0, -6.0])


def pack_weight(w, fmt):
    k, n = w.shape
    w = f64(np.asarray(w, np.float32).astype(ml_dtypes.bfloat16)).reshape(k // 32, 32, n)
    amax = np.abs(w).max(1)
    if fmt == "e4m3":
        byte = np.frexp(amax)[1] - 1 + 127 - 7
    else:
        mant, ex = np.frexp(amax / 6.0)
        byte = np.where(mant > 0.5, ex, ex - 1) + 127
    byte = np.clip(np.where(amax > 0, byte, 1), 1, 254)
    scaled = (w * np.exp2(127.0 - byte)[:, None, :]).reshape(k, n).astype(np.float32)
    by_word = np.ascontiguousarray(scaled.reshape(k // 512, 128, 4, n).transpose(0, 1, 3, 2))
    if fmt == "e4m3":
        words = by_word.astype(ml_dtypes.float8_e4m3fn).view(np.uint8)
    else:
        c = by_word.astype(ml_dtypes.float4_e2m1fn).view(np.uint8) & 0xF
        words = (c[..., 0::2] | (c[..., 1::2] << 4)).reshape(k // 512, 128, 2 * n)
    return np.ascontiguousarray(words), np.ascontiguousarray(byte.astype(np.uint8).reshape(k // 512, 16, n))


def unpack_weight(words, scales, fmt):
    g, _, n = scales.shape
    words = np.ascontiguousarray(words).reshape(g, 128, n, -1)
    if fmt == "e4m3":
        vals = words.view(ml_dtypes.float8_e4m3fn).astype(np.float64)
    else:
        nib = np.empty((g, 128, n, 4), np.uint8)
        nib[..., 0::2] = words & 0xF
        nib[..., 1::2] = words >> 4
        vals = E2M1[nib]
    vals = vals * np.repeat(np.exp2(scales.astype(np.float64) - 127.0), 8, axis=1)[..., None]
    return vals.transpose(0, 1, 3, 2).reshape(g * 512, n)


def sigmoid(v):
    return 1.0 / (1.0 + np.exp(-v))


D, T, I, Q, E = 512, 2048, 512, 256, 512


def setup_inputs():
    n = np.random.standard_normal
    idx = np.random.permutation(T)[:I]
    fd = mx_kscale(D)
    fi = mx_kscale(I)
    keysp = pack_weight(n((D, T)) / fd[:, None], "e4m3")
    return {
        "query": (n((D, Q)) * 1.0 / np.sqrt(D) * fd[:, None]).astype(np.float32),
        "keys_words": keysp[0],
        "keys_scales": keysp[1],
        "bias": (np.random.uniform(-1.0, 1.0, (I, 1))).astype(np.float32),
        "vals": (n((E, T)) * np.random.uniform(0.3, 2.0, (1, T))).astype(np.float32),
        "us": (np.random.uniform(0.02, 0.1, (I, 1)) * fi[:, None]).astype(np.float32),
        "vsc": (np.random.uniform(0.5, 2.0, (I, 1)) / fi[:, None]).astype(np.float32),
        "offs": striped(idx),
    }


def reference(query, keys_words, keys_scales, bias, vals, us, vsc, offs):
    idx = unstriped(offs)
    keysu = unpack_weight(keys_words, keys_scales, "e4m3")
    keysidxg = keysu[:, idx]
    queryq = mxq(f64(query), 0, "e4m3")
    a = keysidxg.T @ queryq
    vt = f64(vals)[:, idx].T
    w = sigmoid(a + f64(bias)) * np.sqrt(np.mean(np.square(vt), axis=1, keepdims=True)) * f64(us)
    vv = vt * f64(vsc)
    wq = mxq(w, 0, "e4m3")
    vvq = mxq(vv, 0, "e4m3")
    o = wq.T @ vvq
    return o

@@ -1,0 +1,225 @@
+from contextlib import ExitStack
+
+import concourse.mybir as mybir
+from concourse.masks import make_identity
+
+D, T, I, Q, E = 512, 2048, 512, 256, 512
+FLOPS = 2 * I * D * Q + 2 * Q * I * E
+
+F32 = mybir.dt.float32
+BF16 = mybir.dt.bfloat16
+I32 = mybir.dt.int32
+U32 = mybir.dt.uint32
+U16 = mybir.dt.uint16
+U8 = mybir.dt.uint8
+FP8X4 = mybir.dt.float8_e4m3fn_x4
+ACT = mybir.ActivationFunctionType
+ALU = mybir.AluOpType
+AXIS = mybir.AxisListType
+
+P = 128
+PACK = 4
+E_BLOCKS = E // P
+Q_TILES = Q // P
+
+
+def tile_attend_valuelength_kernel(tc, query, keys_words, keys_scales, bias, vals, us, vsc, offs, out):
+    nc = tc.nc
+    with ExitStack() as ctx:
+        keep = ctx.enter_context(tc.tile_pool(name="keep", bufs=1))
+        psum = ctx.enter_context(tc.psum_pool(name="psum", bufs=1))
+
+        def sb(name, shape, dtype, tag=None):
+            return keep.tile(shape, dtype, name=name, tag=tag or name, align_bytes=64)
+
+        def bank(tag, name, shape):
+            return psum.tile(shape, F32, name=name, tag=tag)
+
+        offsets = keep.tile([P, I // 16], U16, name="offsets")
+        nc.sync.dma_start(offsets[:], offs)
+        q_raw = sb("q_raw", [P, PACK, Q], F32)
+        nc.sync.dma_start(q_raw[:], query.rearrange("(p j) q -> p j q", j=PACK))
+        slot_cols = {}
+
+        def load_slot_column(name, vec):
+            col = sb(name + "_col", [P, PACK], F32)
+            nc.sync.dma_start(col[:], vec.rearrange("(p t) o -> p (t o)", t=PACK))
+            slot_cols[name] = col
+
+        load_slot_column("vsc", vsc)
+        key_scale_pool = sb("key_scale_pool", [P, T], U8)
+        nc.vector.memset(key_scale_pool[:].bitcast(I32), 0)
+        for quad in range(4):
+            nc.sync.dma_start(
+                key_scale_pool[32 * quad : 32 * quad + 4, :].bitcast(I32),
+                keys_scales[0, 4 * quad : 4 * quad + 4, :].bitcast(I32),
+            )
+        key_pool = sb("key_pool", [P, T], U32)
+        nc.sync.dma_start(key_pool[:].bitcast(I32), keys_words[0].rearrange("p n r -> p (n r)").bitcast(I32))
+        val_pool = []
+
+        def load_values(b):
+            rows = sb("val_pool%d" % b, [P, T], F32)
+            nc.sync.dma_start(rows[:], vals[b * P : (b + 1) * P, :])
+            val_pool.append(rows)
+
+        load_slot_column("bias", bias)
+        load_values(0)
+        load_values(1)
+        load_slot_column("us", us)
+        load_values(2)
+        load_values(3)
+        ident = sb("ident", [P, P], F32)
+        make_identity(nc, ident[:])
+
+        gate_warm = sb("gate_warm", [P, 1], F32)
+        nc.scalar.activation(gate_warm[:], ident[:, 0:1], ACT.Sigmoid)
+        q_bf = sb("q_bf", [P, Q, PACK], BF16)
+        nc.scalar.copy(
+            q_bf[:].rearrange("p (c i) t -> p c t i", i=4),
+            q_raw[:].rearrange("p t (c i) -> p c t i", i=4),
+        )
+        spread = bank("turn0", "spread", [P, PACK, P])
+        for t in range(PACK):
+            nc.tensor.transpose(spread[:, t, :], slot_cols["vsc"][:, t : t + 1].to_broadcast([P, P]), ident[:])
+        vsc_row = sb("vsc_row", [P, I], F32)
+        nc.scalar.copy(vsc_row[:].rearrange("p (s t) -> p s t", t=PACK), spread[:].rearrange("p t s -> p s t"))
+
+        key_scale_listed = sb("key_scale_listed", [P, I], U8)
+        nc.vector.tensor_copy(key_scale_listed[:], key_scale_pool[:].indirect(offsets[:]))
+        q_codes = sb("q_codes", [P, Q], U32, tag="key_scale_pool")
+        q_scales = sb("q_scales", [P, Q], U8)
+        nc.vector.quantize_mx(q_codes[:].bitcast(FP8X4), q_scales[:], q_bf[:].rearrange("p q t -> p (q t)"))
+        key_scales = sb("key_scales", [P, I], U8)
+        nc.vector.tensor_copy(
+            key_scales[:].rearrange("p (t s) -> p s t", t=PACK),
+            key_scale_listed[:].rearrange("p (s t) -> p s t", t=PACK),
+        )
+        key_codes = sb("key_codes", [P, I], U32)
+        nc.vector.tensor_copy(key_codes[:].rearrange("p (t s) -> p s t", t=PACK), key_pool[:].indirect(offsets[:]))
+
+        gate_planes = sb("gate_planes", [P, PACK, Q], F32)
+        for pair in range(2):
+            scores = bank("wide%d" % pair, "scores%d" % pair, [P, 2, Q])
+            for k in range(2):
+                cols = slice((2 * pair + k) * P, (2 * pair + k + 1) * P)
+                nc.tensor.matmul_mx(
+                    out=scores[:, k, :],
+                    lhsT=key_codes[:, cols].bitcast(FP8X4),
+                    lhsT_scale=key_scales[:, cols],
+                    rhs=q_codes[:].bitcast(FP8X4),
+                    rhs_scale=q_scales[:],
+                    start=True,
+                    stop=True,
+                )
+            for k in range(2):
+                t = 2 * pair + k
+                nc.scalar.activation(
+                    gate_planes[:, t, :], scores[:, k, :], ACT.Sigmoid, bias=slot_cols["bias"][:, t : t + 1]
+                )
+        root_warm = sb("root_warm", [P, 1], F32)
+        gate = sb("gate", [P, Q, PACK], F32)
+
+        square_sums = [bank("acc%d" % t, "square_sums%d" % t, [P, P]) for t in range(PACK)]
+        woven = sb("woven", [P, E, PACK], BF16)
+
+        def weave_values(b, turned):
+            nc.scalar.copy(
+                woven[:, b * P : (b + 1) * P, :].rearrange("p e t -> p (e t)").bitcast(F32).rearrange("p (e u) -> p e u", u=2),
+                turned[:].rearrange("p u e -> p e u"),
+            )
+
+        def quantize_values(cols):
+            nc.vector.quantize_mx(
+                v_codes[:, cols].bitcast(FP8X4), v_scales[:, cols], woven[:, cols, :].rearrange("p e t -> p (e t)")
+            )
+
+        for b in range(E_BLOCKS):
+            listed = sb("listed%d" % b, [P, I], F32)
+            squares = sb("squares%d" % b, [P, PACK, P], F32)
+            pieces = 2 if b == E_BLOCKS - 1 else 1
+            n = I // pieces
+            for piece in range(pieces):
+                slots = slice(piece * n, (piece + 1) * n)
+                nc.vector.tensor_copy(
+                    listed[:, slots], val_pool[b][:].indirect(offsets[:, piece * n // 16 : (piece + 1) * n // 16])
+                )
+                nc.scalar.activation(
+                    squares[:, :, piece * n // PACK : (piece + 1) * n // PACK].rearrange("p t s -> p s t"),
+                    listed[:, slots].rearrange("p (s t) -> p s t", t=PACK),
+                    ACT.Square,
+                )
+            scaled = sb("scaled%d" % b, [P, I], BF16)
+            nc.vector.tensor_tensor(scaled[:], listed[:], vsc_row[:], ALU.mult)
+            if b == E_BLOCKS - 1:
+                v_codes = sb("v_codes", [P, E], U32, tag="val_pool%d" % b)
+                v_scales = sb("v_scales", [P, E], U8)
+                quantize_values(slice(0, 2 * P))
+                quantize_values(slice(2 * P, 3 * P))
+            for t in range(PACK):
+                nc.tensor.matmul(
+                    square_sums[t][:],
+                    lhsT=squares[:, t, :],
+                    rhs=ident[:],
+                    start=(b == 0),
+                    stop=(b == E_BLOCKS - 1),
+                    is_transpose=True,
+                )
+            pairs = scaled[:].bitcast(F32)
+            turned = bank("turn%d" % ((b + 1) % 2), "turned%d" % b, [P, 2, P])
+            for u in range(2):
+                nc.tensor.transpose(turned[:, u, :], pairs[:, u::2], ident[:])
+            if b == E_BLOCKS - 1:
+                sums = sb("sums", [P, PACK], F32)
+                spent = sb("spent", [P, 2, P], F32)
+                for t in range(2):
+                    nc.vector.tensor_reduce(sums[:, t : t + 1], square_sums[t][:], AXIS.X, ALU.add)
+                    nc.scalar.activation(
+                        spent[:, t, :], square_sums[t + 2][:], ACT.Copy, accum_out=sums[:, t + 2 : t + 3]
+                    )
+                rms = sb("rms", [P, PACK], F32)
+                nc.scalar.activation(rms[:], sums[:], ACT.Sqrt, scale=1.0 / E)
+            weave_values(b, turned)
+            if b == 0:
+                nc.scalar.activation(root_warm[:], gate_planes[:, PACK - 1, 0:1], ACT.Sqrt)
+            if b == 1:
+                nc.scalar.copy(
+                    gate[:].rearrange("p (c i) t -> p c t i", i=4),
+                    gate_planes[:].rearrange("p t (c i) -> p c t i", i=4),
+                )
+
+        factor = sb("factor", [P, PACK], F32)
+        nc.vector.tensor_tensor(factor[:], rms[:], slot_cols["us"][:], ALU.mult)
+        quantize_values(slice(3 * P, E))
+        w_bf, w_codes, w_scales = [], [], []
+        for h in range(Q_TILES):
+            w_bf.append(sb("w_bf%d" % h, [P, P, PACK], BF16))
+            w_codes.append(sb("w_codes%d" % h, [P, P], U32))
+            w_scales.append(sb("w_scales%d" % h, [P, P], U8))
+        for h in range(Q_TILES):
+            nc.vector.tensor_tensor(
+                w_bf[h][:], gate[:, h * P : (h + 1) * P, :], factor[:].unsqueeze(1).to_broadcast([P, P, PACK]), ALU.mult
+            )
+            nc.vector.quantize_mx(
+                w_codes[h][:].bitcast(FP8X4), w_scales[h][:], w_bf[h][:].rearrange("p q t -> p (q t)")
+            )
+        parts = (
+            (0, slice(0, E), "wide0", nc.scalar.copy, nc.sync),
+            (1, slice(0, E // 2), "wide1", nc.vector.tensor_copy, nc.sync),
+            (1, slice(E // 2, E), "turn1", nc.scalar.copy, nc.scalar),
+        )
+        for n, (h, cols, tag, copy, queue) in enumerate(parts):
+            width = cols.stop - cols.start
+            acc = bank(tag, "product%d" % n, [P, width])
+            nc.tensor.matmul_mx(
+                out=acc[:],
+                lhsT=w_codes[h][:].bitcast(FP8X4),
+                lhsT_scale=w_scales[h][:],
+                rhs=v_codes[:, cols].bitcast(FP8X4),
+                rhs_scale=v_scales[:, cols],
+                start=True,
+                stop=True,
+            )
+            result = sb("result%d" % n, [P, width], F32)
+            copy(result[:], acc[:])
+            queue.dma_start(out[h * P : (h + 1) * P, cols], result[:])

@@ -64,9 +64,9 @@ def tile_attend_valuelength_kernel(tc, query, keys_words, keys_scales, bias, val
             val_pool.append(rows)
 
         load_slot_column("bias", bias)
+        load_slot_column("us", us)
         load_values(0)
         load_values(1)
-        load_slot_column("us", us)
         load_values(2)
         load_values(3)
         ident = sb("ident", [P, P], F32)
@@ -117,11 +117,21 @@ def tile_attend_valuelength_kernel(tc, query, keys_words, keys_scales, bias, val
                 nc.scalar.activation(
                     gate_planes[:, t, :], scores[:, k, :], ACT.Sigmoid, bias=slot_cols["bias"][:, t : t + 1]
                 )
+        gate_scaled = sb("gate_scaled", [P, PACK, Q], F32)
+        for t in range(PACK):
+            nc.gpsimd.tensor_scalar(
+                gate_scaled[:, t, :], gate_planes[:, t, :], slot_cols["us"][:, t : t + 1], 0.0, ALU.mult, ALU.add
+            )
         root_warm = sb("root_warm", [P, 1], F32)
-        gate = sb("gate", [P, Q, PACK], F32)
+        gates = []
 
         square_sums = [bank("acc%d" % t, "square_sums%d" % t, [P, P]) for t in range(PACK)]
         woven = sb("woven", [P, E, PACK], BF16)
+
+        def turn_pairs(turned, scaled):
+            pairs = scaled[:].bitcast(F32)
+            for u in range(2):
+                nc.tensor.transpose(turned[:, u, :], pairs[:, u::2], ident[:])
 
         def weave_values(b, turned):
             nc.scalar.copy(
@@ -156,6 +166,9 @@ def tile_attend_valuelength_kernel(tc, query, keys_words, keys_scales, bias, val
                 v_scales = sb("v_scales", [P, E], U8)
                 quantize_values(slice(0, 2 * P))
                 quantize_values(slice(2 * P, 3 * P))
+            turned = bank("turn%d" % ((b + 1) % 2), "turned%d" % b, [P, 2, P])
+            if b < E_BLOCKS - 1:
+                turn_pairs(turned, scaled)
             for t in range(PACK):
                 nc.tensor.matmul(
                     square_sums[t][:],
@@ -165,32 +178,30 @@ def tile_attend_valuelength_kernel(tc, query, keys_words, keys_scales, bias, val
                     stop=(b == E_BLOCKS - 1),
                     is_transpose=True,
                 )
-            pairs = scaled[:].bitcast(F32)
-            turned = bank("turn%d" % ((b + 1) % 2), "turned%d" % b, [P, 2, P])
-            for u in range(2):
-                nc.tensor.transpose(turned[:, u, :], pairs[:, u::2], ident[:])
+            if b == E_BLOCKS - 1:
+                turn_pairs(turned, scaled)
             if b == E_BLOCKS - 1:
                 sums = sb("sums", [P, PACK], F32)
                 spent = sb("spent", [P, 2, P], F32)
-                for t in range(2):
+                for k in range(2):
+                    t = 2 * k
                     nc.vector.tensor_reduce(sums[:, t : t + 1], square_sums[t][:], AXIS.X, ALU.add)
                     nc.scalar.activation(
-                        spent[:, t, :], square_sums[t + 2][:], ACT.Copy, accum_out=sums[:, t + 2 : t + 3]
+                        spent[:, k, :], square_sums[t + 1][:], ACT.Copy, accum_out=sums[:, t + 1 : t + 2]
                     )
                 rms = sb("rms", [P, PACK], F32)
                 nc.scalar.activation(rms[:], sums[:], ACT.Sqrt, scale=1.0 / E)
             weave_values(b, turned)
             if b == 0:
                 nc.scalar.activation(root_warm[:], gate_planes[:, PACK - 1, 0:1], ACT.Sqrt)
-            if b == 1:
-                nc.scalar.copy(
+            if 1 <= b <= Q_TILES:
+                gate = sb("gate%d" % b, [P, P, PACK], F32, tag="val_pool%d" % b)
+                nc.vector.tensor_copy(
                     gate[:].rearrange("p (c i) t -> p c t i", i=4),
-                    gate_planes[:].rearrange("p t (c i) -> p c t i", i=4),
+                    gate_scaled[:, :, (b - 1) * P : b * P].rearrange("p t (c i) -> p c t i", i=4),
                 )
+                gates.append(gate)
 
-        factor = sb("factor", [P, PACK], F32)
-        nc.vector.tensor_tensor(factor[:], rms[:], slot_cols["us"][:], ALU.mult)
-        quantize_values(slice(3 * P, E))
         w_bf, w_codes, w_scales = [], [], []
         for h in range(Q_TILES):
             w_bf.append(sb("w_bf%d" % h, [P, P, PACK], BF16))
@@ -198,8 +209,10 @@ def tile_attend_valuelength_kernel(tc, query, keys_words, keys_scales, bias, val
             w_scales.append(sb("w_scales%d" % h, [P, P], U8))
         for h in range(Q_TILES):
             nc.vector.tensor_tensor(
-                w_bf[h][:], gate[:, h * P : (h + 1) * P, :], factor[:].unsqueeze(1).to_broadcast([P, P, PACK]), ALU.mult
+                w_bf[h][:], gates[h][:], rms[:].unsqueeze(1).to_broadcast([P, P, PACK]), ALU.mult
             )
+            if h == 0:
+                quantize_values(slice(3 * P, E))
             nc.vector.quantize_mx(
                 w_codes[h][:].bitcast(FP8X4), w_scales[h][:], w_bf[h][:].rearrange("p q t -> p (q t)")
             )

@@ -36,9 +36,9 @@ def tile_attend_valuelength_kernel(tc, query, keys_words, keys_scales, bias, val
             return psum.tile(shape, F32, name=name, tag=tag)
 
         offsets = keep.tile([P, I // 16], U16, name="offsets")
-        nc.sync.dma_start(offsets[:], offs)
         q_raw = sb("q_raw", [P, PACK, Q], F32)
         nc.sync.dma_start(q_raw[:], query.rearrange("(p j) q -> p j q", j=PACK))
+        nc.sync.dma_start(offsets[:], offs)
         slot_cols = {}
 
         def load_slot_column(name, vec):
@@ -123,25 +123,32 @@ def tile_attend_valuelength_kernel(tc, query, keys_words, keys_scales, bias, val
                 gate_scaled[:, t, :], gate_planes[:, t, :], slot_cols["us"][:, t : t + 1], 0.0, ALU.mult, ALU.add
             )
         root_warm = sb("root_warm", [P, 1], F32)
-        gates = []
+        gates = {}
+
+        def weave_gate(h, copy, tag):
+            gates[h] = sb("gate%d" % h, [P, P, PACK], F32, tag=tag)
+            copy(
+                gates[h][:].rearrange("p (c i) t -> p c t i", i=4),
+                gate_scaled[:, :, h * P : (h + 1) * P].rearrange("p t (c i) -> p c t i", i=4),
+            )
 
         square_sums = [bank("acc%d" % t, "square_sums%d" % t, [P, P]) for t in range(PACK)]
-        woven = sb("woven", [P, E, PACK], BF16)
+        woven = sb("woven", [P, E - P, PACK], BF16)
 
         def turn_pairs(turned, scaled):
             pairs = scaled[:].bitcast(F32)
             for u in range(2):
                 nc.tensor.transpose(turned[:, u, :], pairs[:, u::2], ident[:])
 
-        def weave_values(b, turned):
+        def weave_values(target, turned):
             nc.scalar.copy(
-                woven[:, b * P : (b + 1) * P, :].rearrange("p e t -> p (e t)").bitcast(F32).rearrange("p (e u) -> p e u", u=2),
+                target.rearrange("p e t -> p (e t)").bitcast(F32).rearrange("p (e u) -> p e u", u=2),
                 turned[:].rearrange("p u e -> p e u"),
             )
 
-        def quantize_values(cols):
+        def quantize_values(cols, source):
             nc.vector.quantize_mx(
-                v_codes[:, cols].bitcast(FP8X4), v_scales[:, cols], woven[:, cols, :].rearrange("p e t -> p (e t)")
+                v_codes[:, cols].bitcast(FP8X4), v_scales[:, cols], source.rearrange("p e t -> p (e t)")
             )
 
         for b in range(E_BLOCKS):
@@ -164,8 +171,8 @@ def tile_attend_valuelength_kernel(tc, query, keys_words, keys_scales, bias, val
             if b == E_BLOCKS - 1:
                 v_codes = sb("v_codes", [P, E], U32, tag="val_pool%d" % b)
                 v_scales = sb("v_scales", [P, E], U8)
-                quantize_values(slice(0, 2 * P))
-                quantize_values(slice(2 * P, 3 * P))
+                quantize_values(slice(0, 2 * P), woven[:, 0 : 2 * P, :])
+                quantize_values(slice(2 * P, 3 * P), woven[:, 2 * P : 3 * P, :])
             turned = bank("turn%d" % ((b + 1) % 2), "turned%d" % b, [P, 2, P])
             if b < E_BLOCKS - 1:
                 turn_pairs(turned, scaled)
@@ -191,31 +198,43 @@ def tile_attend_valuelength_kernel(tc, query, keys_words, keys_scales, bias, val
                     )
                 rms = sb("rms", [P, PACK], F32)
                 nc.scalar.activation(rms[:], sums[:], ACT.Sqrt, scale=1.0 / E)
-            weave_values(b, turned)
+                woven_last = sb("woven_last", [P, P, PACK], BF16, tag="sums")
+                weave_values(woven_last[:], turned)
+            else:
+                weave_values(woven[:, b * P : (b + 1) * P, :], turned)
             if b == 0:
                 nc.scalar.activation(root_warm[:], gate_planes[:, PACK - 1, 0:1], ACT.Sqrt)
-            if 1 <= b <= Q_TILES:
-                gate = sb("gate%d" % b, [P, P, PACK], F32, tag="val_pool%d" % b)
-                nc.vector.tensor_copy(
-                    gate[:].rearrange("p (c i) t -> p c t i", i=4),
-                    gate_scaled[:, :, (b - 1) * P : b * P].rearrange("p t (c i) -> p c t i", i=4),
-                )
-                gates.append(gate)
+                weave_gate(0, nc.scalar.copy, "gate0")
+            if b == 1:
+                weave_gate(1, nc.vector.tensor_copy, "val_pool1")
 
         w_bf, w_codes, w_scales = [], [], []
         for h in range(Q_TILES):
             w_bf.append(sb("w_bf%d" % h, [P, P, PACK], BF16))
             w_codes.append(sb("w_codes%d" % h, [P, P], U32))
             w_scales.append(sb("w_scales%d" % h, [P, P], U8))
-        for h in range(Q_TILES):
+
+        def weigh(h, rows):
+            width = rows.stop - rows.start
             nc.vector.tensor_tensor(
-                w_bf[h][:], gates[h][:], rms[:].unsqueeze(1).to_broadcast([P, P, PACK]), ALU.mult
+                w_bf[h][:, rows, :], gates[h][:, rows, :], rms[:].unsqueeze(1).to_broadcast([P, width, PACK]), ALU.mult
             )
-            if h == 0:
-                quantize_values(slice(3 * P, E))
+
+        def quantize_weights(h, rows):
             nc.vector.quantize_mx(
-                w_codes[h][:].bitcast(FP8X4), w_scales[h][:], w_bf[h][:].rearrange("p q t -> p (q t)")
+                w_codes[h][:, rows].bitcast(FP8X4),
+                w_scales[h][:, rows],
+                w_bf[h][:, rows, :].rearrange("p q t -> p (q t)"),
             )
+
+        whole, low, high = slice(0, P), slice(0, P // 2), slice(P // 2, P)
+        weigh(0, whole)
+        weigh(1, low)
+        quantize_weights(0, whole)
+        quantize_values(slice(3 * P, E), woven_last[:])
+        weigh(1, high)
+        quantize_weights(1, low)
+        quantize_weights(1, high)
         parts = (
             (0, slice(0, E), "wide0", nc.scalar.copy, nc.sync),
             (1, slice(0, E // 2), "wide1", nc.vector.tensor_copy, nc.sync),

@@ -64,8 +64,8 @@ def tile_attend_valuelength_kernel(tc, query, keys_words, keys_scales, bias, val
             val_pool.append(rows)
 
         load_slot_column("bias", bias)
-        load_slot_column("us", us)
         load_values(0)
+        load_slot_column("us", us)
         load_values(1)
         load_values(2)
         load_values(3)
@@ -125,9 +125,9 @@ def tile_attend_valuelength_kernel(tc, query, keys_words, keys_scales, bias, val
         root_warm = sb("root_warm", [P, 1], F32)
         gates = {}
 
-        def weave_gate(h, copy, tag):
+        def weave_gate(h, tag):
             gates[h] = sb("gate%d" % h, [P, P, PACK], F32, tag=tag)
-            copy(
+            nc.vector.tensor_copy(
                 gates[h][:].rearrange("p (c i) t -> p c t i", i=4),
                 gate_scaled[:, :, h * P : (h + 1) * P].rearrange("p t (c i) -> p c t i", i=4),
             )
@@ -196,6 +196,7 @@ def tile_attend_valuelength_kernel(tc, query, keys_words, keys_scales, bias, val
                     nc.scalar.activation(
                         spent[:, k, :], square_sums[t + 1][:], ACT.Copy, accum_out=sums[:, t + 1 : t + 2]
                     )
+                weave_gate(1, "squares%d" % b)
                 rms = sb("rms", [P, PACK], F32)
                 nc.scalar.activation(rms[:], sums[:], ACT.Sqrt, scale=1.0 / E)
                 woven_last = sb("woven_last", [P, P, PACK], BF16, tag="sums")
@@ -204,9 +205,8 @@ def tile_attend_valuelength_kernel(tc, query, keys_words, keys_scales, bias, val
                 weave_values(woven[:, b * P : (b + 1) * P, :], turned)
             if b == 0:
                 nc.scalar.activation(root_warm[:], gate_planes[:, PACK - 1, 0:1], ACT.Sqrt)
-                weave_gate(0, nc.scalar.copy, "gate0")
             if b == 1:
-                weave_gate(1, nc.vector.tensor_copy, "val_pool1")
+                weave_gate(0, "val_pool1")
 
         w_bf, w_codes, w_scales = [], [], []
         for h in range(Q_TILES):

from contextlib import ExitStack

import concourse.mybir as mybir
from concourse.masks import make_identity

D, T, I, Q, E = 512, 2048, 512, 256, 512
FLOPS = 2 * I * D * Q + 2 * Q * I * E

F32 = mybir.dt.float32
BF16 = mybir.dt.bfloat16
I32 = mybir.dt.int32
U32 = mybir.dt.uint32
U16 = mybir.dt.uint16
U8 = mybir.dt.uint8
FP8X4 = mybir.dt.float8_e4m3fn_x4
ACT = mybir.ActivationFunctionType
ALU = mybir.AluOpType
AXIS = mybir.AxisListType

P = 128
PACK = 4
E_BLOCKS = E // P
Q_TILES = Q // P


def tile_attend_valuelength_kernel(tc, query, keys_words, keys_scales, bias, vals, us, vsc, offs, out):
    nc = tc.nc
    with ExitStack() as ctx:
        keep = ctx.enter_context(tc.tile_pool(name="keep", bufs=1))
        psum = ctx.enter_context(tc.psum_pool(name="psum", bufs=1))

        def sb(name, shape, dtype, tag=None):
            return keep.tile(shape, dtype, name=name, tag=tag or name, align_bytes=64)

        def bank(tag, name, shape):
            return psum.tile(shape, F32, name=name, tag=tag)

        offsets = keep.tile([P, I // 16], U16, name="offsets")
        q_raw = sb("q_raw", [P, PACK, Q], F32)
        nc.sync.dma_start(q_raw[:], query.rearrange("(p j) q -> p j q", j=PACK))
        nc.sync.dma_start(offsets[:], offs)
        slot_cols = {}

        def load_slot_column(name, vec):
            col = sb(name + "_col", [P, PACK], F32)
            nc.sync.dma_start(col[:], vec.rearrange("(p t) o -> p (t o)", t=PACK))
            slot_cols[name] = col

        load_slot_column("vsc", vsc)
        key_scale_pool = sb("key_scale_pool", [P, T], U8)
        nc.vector.memset(key_scale_pool[:].bitcast(I32), 0)
        for quad in range(4):
            nc.sync.dma_start(
                key_scale_pool[32 * quad : 32 * quad + 4, :].bitcast(I32),
                keys_scales[0, 4 * quad : 4 * quad + 4, :].bitcast(I32),
            )
        key_pool = sb("key_pool", [P, T], U32)
        nc.sync.dma_start(key_pool[:].bitcast(I32), keys_words[0].rearrange("p n r -> p (n r)").bitcast(I32))
        val_pool = []

        def load_values(b):
            rows = sb("val_pool%d" % b, [P, T], F32)
            nc.sync.dma_start(rows[:], vals[b * P : (b + 1) * P, :])
            val_pool.append(rows)

        load_slot_column("bias", bias)
        load_values(0)
        load_slot_column("us", us)
        load_values(1)
        load_values(2)
        load_values(3)
        ident = sb("ident", [P, P], F32)
        make_identity(nc, ident[:])

        gate_warm = sb("gate_warm", [P, 1], F32)
        nc.scalar.activation(gate_warm[:], ident[:, 0:1], ACT.Sigmoid)
        q_bf = sb("q_bf", [P, Q, PACK], BF16)
        nc.scalar.copy(
            q_bf[:].rearrange("p (c i) t -> p c t i", i=4),
            q_raw[:].rearrange("p t (c i) -> p c t i", i=4),
        )
        spread = bank("turn0", "spread", [P, PACK, P])
        for t in range(PACK):
            nc.tensor.transpose(spread[:, t, :], slot_cols["vsc"][:, t : t + 1].to_broadcast([P, P]), ident[:])
        vsc_row = sb("vsc_row", [P, I], F32)
        nc.scalar.copy(vsc_row[:].rearrange("p (s t) -> p s t", t=PACK), spread[:].rearrange("p t s -> p s t"))

        key_scale_listed = sb("key_scale_listed", [P, I], U8)
        nc.vector.tensor_copy(key_scale_listed[:], key_scale_pool[:].indirect(offsets[:]))
        q_codes = sb("q_codes", [P, Q], U32, tag="key_scale_pool")
        q_scales = sb("q_scales", [P, Q], U8)
        nc.vector.quantize_mx(q_codes[:].bitcast(FP8X4), q_scales[:], q_bf[:].rearrange("p q t -> p (q t)"))
        key_scales = sb("key_scales", [P, I], U8)
        nc.vector.tensor_copy(
            key_scales[:].rearrange("p (t s) -> p s t", t=PACK),
            key_scale_listed[:].rearrange("p (s t) -> p s t", t=PACK),
        )
        key_codes = sb("key_codes", [P, I], U32)
        nc.vector.tensor_copy(key_codes[:].rearrange("p (t s) -> p s t", t=PACK), key_pool[:].indirect(offsets[:]))

        gate_planes = sb("gate_planes", [P, PACK, Q], F32)
        for pair in range(2):
            scores = bank("wide%d" % pair, "scores%d" % pair, [P, 2, Q])
            for k in range(2):
                cols = slice((2 * pair + k) * P, (2 * pair + k + 1) * P)
                nc.tensor.matmul_mx(
                    out=scores[:, k, :],
                    lhsT=key_codes[:, cols].bitcast(FP8X4),
                    lhsT_scale=key_scales[:, cols],
                    rhs=q_codes[:].bitcast(FP8X4),
                    rhs_scale=q_scales[:],
                    start=True,
                    stop=True,
                )
            for k in range(2):
                t = 2 * pair + k
                nc.scalar.activation(
                    gate_planes[:, t, :], scores[:, k, :], ACT.Sigmoid, bias=slot_cols["bias"][:, t : t + 1]
                )
        gate_scaled = sb("gate_scaled", [P, PACK, Q], F32)
        for t in range(PACK):
            nc.gpsimd.tensor_scalar(
                gate_scaled[:, t, :], gate_planes[:, t, :], slot_cols["us"][:, t : t + 1], 0.0, ALU.mult, ALU.add
            )
        root_warm = sb("root_warm", [P, 1], F32)
        gates = {}

        def weave_gate(h, tag):
            gates[h] = sb("gate%d" % h, [P, P, PACK], F32, tag=tag)
            nc.vector.tensor_copy(
                gates[h][:].rearrange("p (c i) t -> p c t i", i=4),
                gate_scaled[:, :, h * P : (h + 1) * P].rearrange("p t (c i) -> p c t i", i=4),
            )

        square_sums = [bank("acc%d" % t, "square_sums%d" % t, [P, P]) for t in range(PACK)]
        woven = sb("woven", [P, E - P, PACK], BF16)

        def turn_pairs(turned, scaled):
            pairs = scaled[:].bitcast(F32)
            for u in range(2):
                nc.tensor.transpose(turned[:, u, :], pairs[:, u::2], ident[:])

        def weave_values(target, turned):
            nc.scalar.copy(
                target.rearrange("p e t -> p (e t)").bitcast(F32).rearrange("p (e u) -> p e u", u=2),
                turned[:].rearrange("p u e -> p e u"),
            )

        def quantize_values(cols, source):
            nc.vector.quantize_mx(
                v_codes[:, cols].bitcast(FP8X4), v_scales[:, cols], source.rearrange("p e t -> p (e t)")
            )

        for b in range(E_BLOCKS):
            listed = sb("listed%d" % b, [P, I], F32)
            squares = sb("squares%d" % b, [P, PACK, P], F32)
            pieces = 2 if b == E_BLOCKS - 1 else 1
            n = I // pieces
            for piece in range(pieces):
                slots = slice(piece * n, (piece + 1) * n)
                nc.vector.tensor_copy(
                    listed[:, slots], val_pool[b][:].indirect(offsets[:, piece * n // 16 : (piece + 1) * n // 16])
                )
                nc.scalar.activation(
                    squares[:, :, piece * n // PACK : (piece + 1) * n // PACK].rearrange("p t s -> p s t"),
                    listed[:, slots].rearrange("p (s t) -> p s t", t=PACK),
                    ACT.Square,
                )
            scaled = sb("scaled%d" % b, [P, I], BF16)
            nc.vector.tensor_tensor(scaled[:], listed[:], vsc_row[:], ALU.mult)
            if b == E_BLOCKS - 1:
                v_codes = sb("v_codes", [P, E], U32, tag="val_pool%d" % b)
                v_scales = sb("v_scales", [P, E], U8)
                quantize_values(slice(0, 2 * P), woven[:, 0 : 2 * P, :])
                quantize_values(slice(2 * P, 3 * P), woven[:, 2 * P : 3 * P, :])
            turned = bank("turn%d" % ((b + 1) % 2), "turned%d" % b, [P, 2, P])
            if b < E_BLOCKS - 1:
                turn_pairs(turned, scaled)
            for t in range(PACK):
                nc.tensor.matmul(
                    square_sums[t][:],
                    lhsT=squares[:, t, :],
                    rhs=ident[:],
                    start=(b == 0),
                    stop=(b == E_BLOCKS - 1),
                    is_transpose=True,
                )
            if b == E_BLOCKS - 1:
                turn_pairs(turned, scaled)
            if b == E_BLOCKS - 1:
                sums = sb("sums", [P, PACK], F32)
                spent = sb("spent", [P, 2, P], F32)
                for k in range(2):
                    t = 2 * k
                    nc.vector.tensor_reduce(sums[:, t : t + 1], square_sums[t][:], AXIS.X, ALU.add)
                    nc.scalar.activation(
                        spent[:, k, :], square_sums[t + 1][:], ACT.Copy, accum_out=sums[:, t + 1 : t + 2]
                    )
                weave_gate(1, "squares%d" % b)
                rms = sb("rms", [P, PACK], F32)
                nc.scalar.activation(rms[:], sums[:], ACT.Sqrt, scale=1.0 / E)
                woven_last = sb("woven_last", [P, P, PACK], BF16, tag="sums")
                weave_values(woven_last[:], turned)
            else:
                weave_values(woven[:, b * P : (b + 1) * P, :], turned)
            if b == 0:
                nc.scalar.activation(root_warm[:], gate_planes[:, PACK - 1, 0:1], ACT.Sqrt)
            if b == 1:
                weave_gate(0, "val_pool1")

        w_bf, w_codes, w_scales = [], [], []
        for h in range(Q_TILES):
            w_bf.append(sb("w_bf%d" % h, [P, P, PACK], BF16))
            w_codes.append(sb("w_codes%d" % h, [P, P], U32))
            w_scales.append(sb("w_scales%d" % h, [P, P], U8))

        def weigh(h, rows):
            width = rows.stop - rows.start
            nc.vector.tensor_tensor(
                w_bf[h][:, rows, :], gates[h][:, rows, :], rms[:].unsqueeze(1).to_broadcast([P, width, PACK]), ALU.mult
            )

        def quantize_weights(h, rows):
            nc.vector.quantize_mx(
                w_codes[h][:, rows].bitcast(FP8X4),
                w_scales[h][:, rows],
                w_bf[h][:, rows, :].rearrange("p q t -> p (q t)"),
            )

        whole, low, high = slice(0, P), slice(0, P // 2), slice(P // 2, P)
        weigh(0, whole)
        weigh(1, low)
        quantize_weights(0, whole)
        quantize_values(slice(3 * P, E), woven_last[:])
        weigh(1, high)
        quantize_weights(1, low)
        quantize_weights(1, high)
        parts = (
            (0, slice(0, E), "wide0", nc.scalar.copy, nc.sync),
            (1, slice(0, E // 2), "wide1", nc.vector.tensor_copy, nc.sync),
            (1, slice(E // 2, E), "turn1", nc.scalar.copy, nc.scalar),
        )
        for n, (h, cols, tag, copy, queue) in enumerate(parts):
            width = cols.stop - cols.start
            acc = bank(tag, "product%d" % n, [P, width])
            nc.tensor.matmul_mx(
                out=acc[:],
                lhsT=w_codes[h][:].bitcast(FP8X4),
                lhsT_scale=w_scales[h][:],
                rhs=v_codes[:, cols].bitcast(FP8X4),
                rhs_scale=v_scales[:, cols],
                start=True,
                stop=True,
            )
            result = sb("result%d" % n, [P, width], F32)
            copy(result[:], acc[:])
            queue.dma_start(out[h * P : (h + 1) * P, cols], result[:])
